import numpy as np
import ml_dtypes


def mxq(x, axis, fmt="e4m3"):
    dtype, down = {"e4m3": (ml_dtypes.float8_e4m3fn, 7), "e5m2": (ml_dtypes.float8_e5m2, 14)}[fmt]
    v = np.moveaxis(np.asarray(x, np.float32).astype(ml_dtypes.bfloat16).astype(np.float64), axis, -1)
    blocks = v.reshape(v.shape[:-1] + (-1, 32))
    amax = np.abs(blocks).max(-1, keepdims=True)
    byte = np.maximum(np.where(amax > 0, np.frexp(amax)[1] - 1 + 127, 0) - down, 1)
    scale = np.exp2(byte - 127.0)
    codes = (blocks / scale).astype(np.float32).astype(dtype).astype(np.float64)
    return np.moveaxis((codes * scale).reshape(v.shape), -1, axis)


WIDE = False


def mx_kscale(k):
    if not WIDE:
        return np.ones(k)
    levels = np.array([10, -10, 5, -5, 0])
    if k % 512:
        return np.exp2(np.random.permutation(np.resize(levels, k // 32))).repeat(32)
    a = np.empty((k // 512, 16))
    for p in range(k // 512):
        a[p, :8] = np.random.permutation(np.resize(levels, 8))
        for g in range(8):
            far = levels[np.abs(levels - a[p, g]) >= 10]
            a[p, g + 8] = far[np.random.randint(len(far))]
    return np.exp2(a.ravel()).repeat(32)


def f64(x):
    return np.asarray(x).astype(np.float64)


def striped(idx):
    return np.tile(idx.reshape(-1, 16).T, (8, 1)).astype(np.uint16)


def unstriped(offs):
    return offs[:16].T.reshape(-1).astype(np.int64)


def striped8(idx):
    return np.concatenate([x.reshape(-1, 16).T for x in idx]).astype(np.uint16)


def runs(offs, k):
    lists = np.stack([offs[16 * r : 16 * r + 16].T.reshape(-1) for r in range(8)]).astype(np.int64)
    return lists[np.arange(k) % 512 // 64]


def pack_weight(w):
    k, n = w.shape
    w = f64(np.asarray(w, np.float32).astype(ml_dtypes.bfloat16)).reshape(k // 32, 32, n)
    amax = np.abs(w).max(1)
    byte = np.clip(np.where(amax > 0, np.frexp(amax)[1] - 1 + 127 - 7, 1), 1, 254)
    scaled = (w * np.exp2(127.0 - byte)[:, None, :]).reshape(k, n).astype(np.float32)
    words = np.ascontiguousarray(scaled.reshape(k // 512, 128, 4, n).transpose(0, 1, 3, 2)).astype(ml_dtypes.float8_e4m3fn).view(np.uint8)
    return words, np.ascontiguousarray(byte.astype(np.uint8).reshape(k // 512, 16, n))


def unpack_weight(words, scales):
    g, p, n, _ = words.shape
    vals = np.ascontiguousarray(words).view(ml_dtypes.float8_e4m3fn).astype(np.float64) * np.repeat(np.exp2(scales.astype(np.float64) - 127.0), 8, axis=1)[..., None]
    return vals.transpose(0, 1, 3, 2).reshape(g * 512, n)

def planes(y):
    n, m = y.shape
    v = y.astype(np.float32).astype(ml_dtypes.bfloat16).astype(np.float64).reshape(n // 32, 32, m)
    top = np.abs(v).max(1)
    byte = np.clip(np.where(top > 0, np.frexp(top)[1] - 1 + 127 - 7, 1), 1, 254)
    codes = (v * np.exp2(127.0 - byte)[:, None, :]).reshape(n, m).astype(np.float32).astype(ml_dtypes.float8_e4m3fn).view(np.uint8)
    words = codes.reshape(n // 512, 128, 4, m).transpose(0, 1, 3, 2)
    return np.ascontiguousarray(words), np.ascontiguousarray(byte.astype(np.uint8).reshape(n // 512, 16, m))


K, T, S, H = 512, 2048, 512, 512


def setup_inputs():
    n = np.random.standard_normal
    s = mx_kscale(K)[:, None]
    u = mx_kscale(S)
    packed_xT = pack_weight(n((K, T)) * s)
    return {
        "x_words": packed_xT[0],
        "x_scales": packed_xT[1],
        "wa": (n((K, H)) / np.sqrt(K) / s).astype(np.float32),
        "wb": (n((K, H)) / np.sqrt(K) / s).astype(np.float32),
        "gt": (np.random.uniform(0.5, 1.5, (S, 1)) * u[:, None]).astype(np.float32),
        "gi": (np.random.uniform(0.5, 1.5, (S, 1)) / u[:, None]).astype(np.float32),
        "offs": striped(np.random.permutation(T)[:S]),
        "two": striped(np.random.permutation(T)[:S]),
        "n1": striped(np.random.permutation(H)),
        "n2": striped(np.random.permutation(H)),
        "n3": striped8(np.stack([np.random.permutation(H) for _ in range(8)])),
        "n4": striped8(np.stack([np.random.permutation(H) for _ in range(8)])),
    }


def reference(x_words, x_scales, wa, wb, gt, gi, offs, two, n1, n2, n3, n4):
    xq = unpack_weight(x_words, x_scales)[:, unstriped(offs)]
    a = xq.T @ mxq(f64(wa), 0, "e4m3")
    x_two = unpack_weight(x_words, x_scales)[:, unstriped(two)]
    b = x_two.T @ mxq(f64(wb), 0, "e4m3")
    z = f64(gt) * (np.maximum(a, b[:, unstriped(n2)]) - (np.minimum(a[:, unstriped(n1)], b)))
    z2 = f64(gi) * b
    cv = 0.0625 * ((mxq(z, 0, "e4m3").T @ mxq(z2, 0, "e4m3")))
    out_0 = np.maximum(cv[np.arange(H)[:, None], runs(n3, H)], cv[np.arange(H)[:, None], runs(n4, H)]) - (0.75 * cv)
    return (out_0,) + planes(out_0)

@@ -1,0 +1,240 @@
+from contextlib import ExitStack
+
+import concourse.mybir as mybir
+from concourse.masks import make_identity
+
+K, T, S, H = 512, 2048, 512, 512
+FLOPS = 2 * K * S * H * 2 + 2 * S * H * H
+
+F32 = mybir.dt.float32
+BF16 = mybir.dt.bfloat16
+I32 = mybir.dt.int32
+U32 = mybir.dt.uint32
+U16 = mybir.dt.uint16
+U8 = mybir.dt.uint8
+FP8X4 = mybir.dt.float8_e4m3fn_x4
+ALU = mybir.AluOpType
+COPY = mybir.ActivationFunctionType.Copy
+
+P = 128
+PACK = 4
+CHUNKS = ((0, 256), (256, 128), (384, 128))
+W_HALF = H // 2
+
+
+def tile_picked_momtmaxbover_none_po_kernel(
+    tc, x_words, x_scales, wa, wb, gt, gi, offs, two, n1, n2, n3, n4, out_0, out_1, out_2
+):
+    nc = tc.nc
+    with ExitStack() as ctx:
+        lists = ctx.enter_context(tc.tile_pool(name="lists", bufs=1))
+        keep = ctx.enter_context(tc.tile_pool(name="keep", bufs=1))
+        psum = ctx.enter_context(tc.psum_pool(name="psum", bufs=1))
+
+        def load_list(name, src):
+            tile = lists.tile([P, S // 16], U16, name=name)
+            nc.sync.dma_start(tile[:], src)
+            return tile
+
+        def load_weight_half(name, w, half):
+            raw = keep.tile([P, PACK, W_HALF], F32, name=name)
+            nc.sync.dma_start(
+                raw[:], w.rearrange("(p j) c -> p j c", j=PACK)[:, :, half * W_HALF : (half + 1) * W_HALF]
+            )
+            return raw
+
+        xs = keep.tile([P, T], U8, name="xs", align_bytes=64)
+        nc.vector.memset(xs[:].bitcast(I32), 0)
+        two_t = load_list("two_t", two)
+        xw = keep.tile([P, T], U32, name="xw", align_bytes=64)
+        nc.sync.dma_start(xw[:].bitcast(I32), x_words[0].rearrange("p n t -> p (n t)").bitcast(I32))
+        for q in range(4):
+            nc.scalar.dma_start(
+                xs[32 * q : 32 * q + 4, :].bitcast(I32), x_scales[0, 4 * q : 4 * q + 4, :].bitcast(I32)
+            )
+        offs_t = load_list("offs_t", offs)
+        wb_raw = [load_weight_half(f"wb_raw{h}", wb, h) for h in range(2)]
+        rows = keep.tile([P, P], F32, name="rows")
+        nc.gpsimd.memset(rows[:], 0.0)
+        for k, g in enumerate((gt, gi)):
+            nc.sync.dma_start(
+                rows[PACK * k : PACK * (k + 1), :].rearrange("t (b r) -> t b r", r=8),
+                g.rearrange("(b t r) o -> t b (r o)", t=PACK, r=8),
+            )
+        wa_raw = [load_weight_half(f"wa_raw{h}", wa, h) for h in range(2)]
+        n2_t = load_list("n2_t", n2)
+        n1_t = load_list("n1_t", n1)
+        n3_t = load_list("n3_t", n3)
+        n4_t = load_list("n4_t", n4)
+
+        ident = keep.tile([P, P], F32, name="ident")
+        make_identity(nc, ident[:])
+        turned = psum.tile([P, P], F32, name="turned", tag="bank7")
+        nc.tensor.transpose(turned[:], rows[:], ident[:])
+        gains = keep.tile([P, 2 * PACK], F32, name="gains")
+        nc.scalar.copy(gains[:], turned[:, 0 : 2 * PACK])
+
+        def pick(name, offsets, words_tag):
+            scales = keep.tile([P, S], U8, name=name + "_scales", align_bytes=64)
+            nc.vector.tensor_copy(
+                scales[:].rearrange("p (t b r) -> p b t r", t=PACK, r=8), xs[:].indirect(offsets[:])
+            )
+            words = keep.tile([P, S], U32, name=name + "_words", tag=words_tag, align_bytes=64)
+            nc.vector.tensor_copy(
+                words[:].rearrange("p (t b r) -> p b t r", t=PACK, r=8), xw[:].indirect(offsets[:])
+            )
+            return words, scales
+
+        def quantise_weight(name, raws, copies):
+            codes = keep.tile([P, H], U32, name=name + "_codes", align_bytes=64)
+            scales = keep.tile([P, H], U8, name=name + "_scales", align_bytes=64)
+            for half in range(2):
+                grouped = keep.tile([P, W_HALF * PACK], BF16, name=f"{name}_grouped{half}", tag=f"{name}_grouped{half}", align_bytes=64)
+                copies[half](
+                    grouped[:].rearrange("p (c i j) -> p c j i", i=4, j=PACK),
+                    raws[half][:].rearrange("p j (c i) -> p c j i", i=4),
+                )
+                cols = slice(half * W_HALF, (half + 1) * W_HALF)
+                nc.vector.quantize_mx(codes[:, cols].bitcast(FP8X4), scales[:, cols], grouped[:])
+            return codes, scales
+
+        def product(name, first_bank, lhs, rhs):
+            banks = []
+            for t in range(PACK):
+                acc = psum.tile([P, H], F32, name=f"{name}{t}", tag=f"bank{first_bank + t}")
+                cols = slice(t * P, (t + 1) * P)
+                nc.tensor.matmul_mx(
+                    out=acc[:],
+                    lhsT=lhs[0][:, cols].bitcast(FP8X4),
+                    lhsT_scale=lhs[1][:, cols],
+                    rhs=rhs[0][:].bitcast(FP8X4),
+                    rhs_scale=rhs[1][:],
+                    start=True,
+                    stop=True,
+                )
+                banks.append(acc)
+            return banks
+
+        x_two = pick("x_two", two_t, "x_two_words")
+        wb_q = quantise_weight("wb", wb_raw, (nc.scalar.copy, nc.scalar.copy))
+        b_ps = product("b_ps", 0, x_two, wb_q)
+        x_idx = pick("x_idx", offs_t, "wb_grouped1")
+        wa_q = quantise_weight("wa", wa_raw, (nc.scalar.copy, nc.vector.tensor_copy))
+        a_ps = product("a_ps", 4, x_idx, wa_q)
+
+        b_all = keep.tile([P, PACK, H], F32, name="b_all")
+        a_all = keep.tile([P, PACK, H], F32, name="a_all")
+        for t in range(PACK):
+            copy = nc.scalar.copy if t < 3 else nc.vector.tensor_copy
+            copy(b_all[:, t, :], b_ps[t][:])
+
+        z2_grouped = keep.tile([P, H * PACK], BF16, name="z2_grouped", align_bytes=64)
+        z2_codes = keep.tile([P, H], U32, name="z2_codes", align_bytes=64)
+        z2_scales = keep.tile([P, H], U8, name="z2_scales", align_bytes=64)
+        nc.vector.tensor_tensor(
+            z2_grouped[:].rearrange("p (c i t) -> p c t i", i=4, t=PACK),
+            b_all[:].rearrange("p t (c i) -> p c t i", i=4),
+            gains[:, PACK : 2 * PACK].unsqueeze(1).unsqueeze(3).to_broadcast([P, H // 4, PACK, 4]),
+            ALU.mult,
+        )
+        nc.vector.quantize_mx(z2_codes[:].bitcast(FP8X4), z2_scales[:], z2_grouped[:])
+
+        z_grouped = keep.tile([P, PACK, P * PACK], BF16, name="z_grouped", align_bytes=64)
+        z_codes = keep.tile([P, H], U32, name="z_codes", align_bytes=64)
+        z_scales = keep.tile([P, H], U8, name="z_scales", align_bytes=64)
+        for c, (first, width) in enumerate(CHUNKS):
+            cols = slice(first, first + width)
+            entries = slice(first // 16, (first + width) // 16)
+            if c == 0:
+                b_at = keep.tile([P, PACK, width], F32, name="b_at", tag="held2")[:]
+                a_at = keep.tile([P, PACK, width], F32, name="a_at")[:]
+            else:
+                if c == 1:
+                    later = keep.tile([P, 2, 2, PACK, width], F32, name="later2", tag="held2")
+                b_at = later[:, c - 1, 0]
+                a_at = later[:, c - 1, 1]
+            for t in range(PACK):
+                nc.scalar.activation(b_at[:, t, :], b_all[:, t, :].indirect(n2_t[:, entries]), COPY)
+            if c == 0:
+                for t in range(PACK):
+                    nc.scalar.copy(a_all[:, t, :], a_ps[t][:])
+            for t in range(PACK):
+                nc.scalar.activation(a_at[:, t, :], a_all[:, t, :].indirect(n1_t[:, entries]), COPY)
+            upper = keep.tile([P, PACK, width], F32, name=f"upper{c}")
+            lower = keep.tile([P, PACK, width], F32, name=f"lower{c}")
+            for t in range(PACK):
+                nc.vector.tensor_tensor(upper[:, t, :], a_ps[t][:, cols], b_at[:, t, :], ALU.max)
+            for t in range(PACK):
+                nc.vector.tensor_tensor(lower[:, t, :], b_ps[t][:, cols], a_at[:, t, :], ALU.min)
+            spread = keep.tile([P, PACK, width], F32, name=f"spread{c}")
+            nc.vector.tensor_tensor(spread[:], upper[:], lower[:], ALU.subtract)
+            nc.vector.tensor_tensor(
+                z_grouped[:, :, cols].rearrange("p u (m t) -> p m t u", t=PACK),
+                spread[:].rearrange("p t (m u) -> p m t u", u=PACK),
+                gains[:, 0:PACK].unsqueeze(1).unsqueeze(3).to_broadcast([P, width // PACK, PACK, PACK]),
+                ALU.mult,
+            )
+            if (first + width) % 256 == 0:
+                half = (first + width) // 256 - 1
+                for u in range(PACK):
+                    words = slice(u * P + 64 * half, u * P + 64 * (half + 1))
+                    nc.vector.quantize_mx(
+                        z_codes[:, words].bitcast(FP8X4),
+                        z_scales[:, words],
+                        z_grouped[:, u, 256 * half : 256 * (half + 1)],
+                    )
+
+        cv_ps = product("cv_ps", 0, (z_codes, z_scales), (z2_codes, z2_scales))
+        cv_win = []
+        for u in range(PACK):
+            win = keep.tile([P, H], F32, name=f"cv_win{u}")
+            if u == 0:
+                nc.scalar.activation(win[:], cv_ps[u][:], COPY, scale=0.0625)
+            else:
+                nc.vector.tensor_scalar(win[:], cv_ps[u][:], 0.0625, None, ALU.mult)
+            cv_win.append(win)
+
+        y_codes = keep.tile([P, H], U32, name="y_codes", align_bytes=64)
+        y_scales = keep.tile([P, H], U8, name="y_scales", align_bytes=64)
+        y_rows = out_0.rearrange("(p u) c -> p u c", u=PACK)
+        y_words = out_1[0].rearrange("p n t -> p (n t)").bitcast(I32)
+        for c, (first, width) in enumerate(CHUNKS):
+            cols = slice(first, first + width)
+            entries = slice(first // 16, (first + width) // 16)
+            if c == 0:
+                early = keep.tile([P, 2, 2, width], F32, name="early3", tag="held3")
+                rest = keep.tile([P, 2, 2, width], F32, name="rest3")
+                at = [[(early if u < 2 else rest)[:, u % 2, k, :] for k in range(2)] for u in range(PACK)]
+            else:
+                if c == 1:
+                    later = keep.tile([P, 2, PACK, 2, width], F32, name="later3", tag="held3")
+                at = [[later[:, c - 1, u, k, :] for k in range(2)] for u in range(PACK)]
+            for u in range(PACK):
+                for k, offsets in enumerate((n3_t, n4_t)):
+                    looked_up = cv_win[u][:].indirect(offsets[:, entries])
+                    if (c == 0 and u == 3) or (c == 2 and u == 0 and k == 0):
+                        nc.vector.tensor_copy(at[u][k], looked_up)
+                    else:
+                        nc.scalar.activation(at[u][k], looked_up, COPY)
+            larger = keep.tile([P, PACK, width], F32, name=f"larger{c}")
+            y = keep.tile([P, PACK, width], F32, name=f"y{c}")
+            for u in range(PACK):
+                nc.vector.tensor_tensor(larger[:, u, :], at[u][0], at[u][1], ALU.max)
+            for u in range(PACK):
+                nc.vector.scalar_tensor_tensor(
+                    y[:, u, :], cv_ps[u][:, cols], -0.75 * 0.0625, larger[:, u, :], ALU.mult, ALU.add
+                )
+            nc.sync.dma_start(y_rows[:, :, cols], y[:])
+            y_grouped = keep.tile([P, width * PACK], BF16, name=f"y_grouped{c}", align_bytes=64)
+            nc.vector.tensor_copy(
+                y_grouped[:].rearrange("p (c i u) -> p c u i", i=4, u=PACK),
+                y[:].rearrange("p u (c i) -> p c u i", i=4),
+            )
+            nc.vector.quantize_mx(y_codes[:, cols].bitcast(FP8X4), y_scales[:, cols], y_grouped[:])
+            engine = nc.scalar if c == len(CHUNKS) - 1 else nc.sync
+            engine.dma_start(y_words[:, cols], y_codes[:, cols].bitcast(I32))
+        for q in range(4):
+            engine = nc.scalar if q % 2 else nc.sync
+            engine.dma_start(
+                out_2[0, 4 * q : 4 * q + 4, :].bitcast(I32), y_scales[32 * q : 32 * q + 4, :].bitcast(I32)
+            )

@@ -18,6 +18,8 @@ COPY = mybir.ActivationFunctionType.Copy
 
 P = 128
 PACK = 4
+QUARTER = 128
+STRIP = 64
 CHUNKS = ((0, 256), (256, 128), (384, 128))
 W_HALF = H // 2
 
@@ -36,32 +38,30 @@ def tile_picked_momtmaxbover_none_po_kernel(
             nc.sync.dma_start(tile[:], src)
             return tile
 
-        def load_weight_half(name, w, half):
-            raw = keep.tile([P, PACK, W_HALF], F32, name=name)
-            nc.sync.dma_start(
-                raw[:], w.rearrange("(p j) c -> p j c", j=PACK)[:, :, half * W_HALF : (half + 1) * W_HALF]
-            )
+        def load_weight(name, w, first, width):
+            raw = keep.tile([P, PACK, width], F32, name=name)
+            nc.sync.dma_start(raw[:], w.rearrange("(p j) c -> p j c", j=PACK)[:, :, first : first + width])
             return raw
 
         xs = keep.tile([P, T], U8, name="xs", align_bytes=64)
         nc.vector.memset(xs[:].bitcast(I32), 0)
-        two_t = load_list("two_t", two)
-        xw = keep.tile([P, T], U32, name="xw", align_bytes=64)
-        nc.sync.dma_start(xw[:].bitcast(I32), x_words[0].rearrange("p n t -> p (n t)").bitcast(I32))
         for q in range(4):
             nc.scalar.dma_start(
                 xs[32 * q : 32 * q + 4, :].bitcast(I32), x_scales[0, 4 * q : 4 * q + 4, :].bitcast(I32)
             )
+        two_t = load_list("two_t", two)
+        xw = keep.tile([P, T], U32, name="xw", align_bytes=64)
+        nc.sync.dma_start(xw[:].bitcast(I32), x_words[0].rearrange("p n t -> p (n t)").bitcast(I32))
+        wb_raw = [load_weight(f"wb_raw{h}", wb, h * W_HALF, W_HALF) for h in range(2)]
         offs_t = load_list("offs_t", offs)
-        wb_raw = [load_weight_half(f"wb_raw{h}", wb, h) for h in range(2)]
+        wa_raw = [load_weight(f"wa_raw{h}", wa, h * W_HALF, W_HALF) for h in range(2)]
         rows = keep.tile([P, P], F32, name="rows")
         nc.gpsimd.memset(rows[:], 0.0)
         for k, g in enumerate((gt, gi)):
-            nc.sync.dma_start(
+            nc.gpsimd.dma_start(
                 rows[PACK * k : PACK * (k + 1), :].rearrange("t (b r) -> t b r", r=8),
                 g.rearrange("(b t r) o -> t b (r o)", t=PACK, r=8),
             )
-        wa_raw = [load_weight_half(f"wa_raw{h}", wa, h) for h in range(2)]
         n2_t = load_list("n2_t", n2)
         n1_t = load_list("n1_t", n1)
         n3_t = load_list("n3_t", n3)
@@ -74,27 +74,24 @@ def tile_picked_momtmaxbover_none_po_kernel(
         gains = keep.tile([P, 2 * PACK], F32, name="gains")
         nc.scalar.copy(gains[:], turned[:, 0 : 2 * PACK])
 
-        def pick(name, offsets, words_tag):
-            scales = keep.tile([P, S], U8, name=name + "_scales", align_bytes=64)
+        def pick(name, table, dtype, offsets, tag):
+            picked = keep.tile([P, S], dtype, name=name, tag=tag, align_bytes=64)
             nc.vector.tensor_copy(
-                scales[:].rearrange("p (t b r) -> p b t r", t=PACK, r=8), xs[:].indirect(offsets[:])
+                picked[:].rearrange("p (t b r) -> p b t r", t=PACK, r=8), table[:].indirect(offsets[:])
             )
-            words = keep.tile([P, S], U32, name=name + "_words", tag=words_tag, align_bytes=64)
-            nc.vector.tensor_copy(
-                words[:].rearrange("p (t b r) -> p b t r", t=PACK, r=8), xw[:].indirect(offsets[:])
-            )
-            return words, scales
+            return picked
 
         def quantise_weight(name, raws, copies):
-            codes = keep.tile([P, H], U32, name=name + "_codes", align_bytes=64)
+            codes = keep.tile([P, H], U32, name=name + "_codes", tag=name + "_codes", align_bytes=64)
             scales = keep.tile([P, H], U8, name=name + "_scales", align_bytes=64)
-            for half in range(2):
-                grouped = keep.tile([P, W_HALF * PACK], BF16, name=f"{name}_grouped{half}", tag=f"{name}_grouped{half}", align_bytes=64)
-                copies[half](
+            width = H // len(raws)
+            for piece, raw in enumerate(raws):
+                grouped = keep.tile([P, width * PACK], BF16, name=f"{name}_grouped{piece}", tag=f"{name}_grouped{piece}", align_bytes=64)
+                copies[piece](
                     grouped[:].rearrange("p (c i j) -> p c j i", i=4, j=PACK),
-                    raws[half][:].rearrange("p j (c i) -> p c j i", i=4),
+                    raw[:].rearrange("p j (c i) -> p c j i", i=4),
                 )
-                cols = slice(half * W_HALF, (half + 1) * W_HALF)
+                cols = slice(piece * width, (piece + 1) * width)
                 nc.vector.quantize_mx(codes[:, cols].bitcast(FP8X4), scales[:, cols], grouped[:])
             return codes, scales
 
@@ -115,83 +112,93 @@ def tile_picked_momtmaxbover_none_po_kernel(
                 banks.append(acc)
             return banks
 
-        x_two = pick("x_two", two_t, "x_two_words")
+        two_scales = pick("two_scales", xs, U8, two_t, "two_scales")
+        two_words = pick("two_words", xw, U32, two_t, "two_words")
+        idx_scales = pick("idx_scales", xs, U8, offs_t, "idx_scales")
         wb_q = quantise_weight("wb", wb_raw, (nc.scalar.copy, nc.scalar.copy))
-        b_ps = product("b_ps", 0, x_two, wb_q)
-        x_idx = pick("x_idx", offs_t, "wb_grouped1")
+        b_ps = product("b_ps", 0, (two_words, two_scales), wb_q)
+        idx_words = pick("idx_words", xw, U32, offs_t, "wb_grouped1")
         wa_q = quantise_weight("wa", wa_raw, (nc.scalar.copy, nc.vector.tensor_copy))
-        a_ps = product("a_ps", 4, x_idx, wa_q)
+        a_ps = product("a_ps", 4, (idx_words, idx_scales), wa_q)
 
         b_all = keep.tile([P, PACK, H], F32, name="b_all")
         a_all = keep.tile([P, PACK, H], F32, name="a_all")
         for t in range(PACK):
-            copy = nc.scalar.copy if t < 3 else nc.vector.tensor_copy
-            copy(b_all[:, t, :], b_ps[t][:])
+            nc.scalar.copy(b_all[:, t, :], b_ps[t][:])
 
         z2_grouped = keep.tile([P, H * PACK], BF16, name="z2_grouped", align_bytes=64)
-        z2_codes = keep.tile([P, H], U32, name="z2_codes", align_bytes=64)
+        z2_codes = keep.tile([P, H], U32, name="z2_codes", tag="z2_codes", align_bytes=64)
         z2_scales = keep.tile([P, H], U8, name="z2_scales", align_bytes=64)
-        nc.vector.tensor_tensor(
-            z2_grouped[:].rearrange("p (c i t) -> p c t i", i=4, t=PACK),
-            b_all[:].rearrange("p t (c i) -> p c t i", i=4),
-            gains[:, PACK : 2 * PACK].unsqueeze(1).unsqueeze(3).to_broadcast([P, H // 4, PACK, 4]),
-            ALU.mult,
-        )
-        nc.vector.quantize_mx(z2_codes[:].bitcast(FP8X4), z2_scales[:], z2_grouped[:])
-
         z_grouped = keep.tile([P, PACK, P * PACK], BF16, name="z_grouped", align_bytes=64)
         z_codes = keep.tile([P, H], U32, name="z_codes", align_bytes=64)
         z_scales = keep.tile([P, H], U8, name="z_scales", align_bytes=64)
-        for c, (first, width) in enumerate(CHUNKS):
-            cols = slice(first, first + width)
-            entries = slice(first // 16, (first + width) // 16)
-            if c == 0:
-                b_at = keep.tile([P, PACK, width], F32, name="b_at", tag="held2")[:]
-                a_at = keep.tile([P, PACK, width], F32, name="a_at")[:]
-            else:
-                if c == 1:
-                    later = keep.tile([P, 2, 2, PACK, width], F32, name="later2", tag="held2")
-                b_at = later[:, c - 1, 0]
-                a_at = later[:, c - 1, 1]
-            for t in range(PACK):
-                nc.scalar.activation(b_at[:, t, :], b_all[:, t, :].indirect(n2_t[:, entries]), COPY)
-            if c == 0:
-                for t in range(PACK):
-                    nc.scalar.copy(a_all[:, t, :], a_ps[t][:])
-            for t in range(PACK):
-                nc.scalar.activation(a_at[:, t, :], a_all[:, t, :].indirect(n1_t[:, entries]), COPY)
-            upper = keep.tile([P, PACK, width], F32, name=f"upper{c}")
-            lower = keep.tile([P, PACK, width], F32, name=f"lower{c}")
-            for t in range(PACK):
-                nc.vector.tensor_tensor(upper[:, t, :], a_ps[t][:, cols], b_at[:, t, :], ALU.max)
-            for t in range(PACK):
-                nc.vector.tensor_tensor(lower[:, t, :], b_ps[t][:, cols], a_at[:, t, :], ALU.min)
-            spread = keep.tile([P, PACK, width], F32, name=f"spread{c}")
-            nc.vector.tensor_tensor(spread[:], upper[:], lower[:], ALU.subtract)
-            nc.vector.tensor_tensor(
-                z_grouped[:, :, cols].rearrange("p u (m t) -> p m t u", t=PACK),
-                spread[:].rearrange("p t (m u) -> p m t u", u=PACK),
-                gains[:, 0:PACK].unsqueeze(1).unsqueeze(3).to_broadcast([P, width // PACK, PACK, PACK]),
+
+        def look_up(out, table, offsets, first, width, slots):
+            for t in slots:
+                entries = offsets[:, first // 16 : (first + width) // 16]
+                nc.scalar.activation(out[:, t, :], table[:, t, :].indirect(entries), COPY)
+
+        def weigh_b(first, width):
+            nc.gpsimd.tensor_tensor(
+                z2_grouped[:, first * PACK : (first + width) * PACK].rearrange("p (c i t) -> p c t i", i=4, t=PACK),
+                b_all[:, :, first : first + width].rearrange("p t (c i) -> p c t i", i=4),
+                gains[:, PACK : 2 * PACK].unsqueeze(1).unsqueeze(3).to_broadcast([P, width // 4, PACK, 4]),
                 ALU.mult,
             )
-            if (first + width) % 256 == 0:
-                half = (first + width) // 256 - 1
-                for u in range(PACK):
-                    words = slice(u * P + 64 * half, u * P + 64 * (half + 1))
-                    nc.vector.quantize_mx(
-                        z_codes[:, words].bitcast(FP8X4),
-                        z_scales[:, words],
-                        z_grouped[:, u, 256 * half : 256 * (half + 1)],
+
+        b_at0 = keep.tile([P, PACK, W_HALF], F32, name="b_at0")
+        look_up(b_at0, b_all, n2_t, 0, W_HALF, range(PACK))
+        weigh_b(0, H)
+        for t in range(PACK):
+            nc.vector.tensor_copy(a_all[:, t, :], a_ps[t][:])
+        b_at1 = keep.tile([P, PACK, W_HALF], F32, name="b_at1", tag="wa_codes", align_bytes=64)
+        for half, b_at in enumerate((b_at0, b_at1)):
+            if half == 1:
+                look_up(b_at1, b_all, n2_t, W_HALF, W_HALF, range(PACK))
+            upper = keep.tile([P, PACK, W_HALF], F32, name=f"upper{half}")
+            cols = slice(half * W_HALF, (half + 1) * W_HALF)
+            if half == 0:
+                for t in range(PACK):
+                    nc.vector.tensor_tensor(upper[:, t, :], a_ps[t][:, cols], b_at[:, t, :], ALU.max)
+            else:
+                nc.vector.tensor_tensor(upper[:], a_all[:, :, cols], b_at[:], ALU.max)
+            if half == 0:
+                nc.vector.quantize_mx(z2_codes[:].bitcast(FP8X4), z2_scales[:], z2_grouped[:])
+            for quarter in range(2):
+                first = half * W_HALF + quarter * QUARTER
+                a_at = keep.tile([P, PACK, QUARTER], F32, name=f"a_at{half}{quarter}")
+                look_up(a_at, a_all, n1_t, first, QUARTER, range(PACK))
+                lower = keep.tile([P, 2, PACK, STRIP], F32, name=f"lower{half}{quarter}")
+                spread = keep.tile([P, 2, PACK, STRIP], F32, name=f"spread{half}{quarter}")
+                for s in range(2):
+                    at = first + s * STRIP
+                    nc.vector.tensor_tensor(
+                        lower[:, s], b_all[:, :, at : at + STRIP], a_at[:, :, s * STRIP : (s + 1) * STRIP], ALU.min
                     )
+                for s in range(2):
+                    at = quarter * QUARTER + s * STRIP
+                    nc.vector.tensor_tensor(spread[:, s], upper[:, :, at : at + STRIP], lower[:, s], ALU.subtract)
+                for s in range(2):
+                    at = first + s * STRIP
+                    nc.vector.tensor_tensor(
+                        z_grouped[:, :, at : at + STRIP].rearrange("p u (m t) -> p m t u", t=PACK),
+                        spread[:, s].rearrange("p t (m u) -> p m t u", u=PACK),
+                        gains[:, 0:PACK].unsqueeze(1).unsqueeze(3).to_broadcast([P, STRIP // PACK, PACK, PACK]),
+                        ALU.mult,
+                    )
+            for u in range(PACK):
+                words = slice(u * P + 64 * half, u * P + 64 * (half + 1))
+                nc.vector.quantize_mx(
+                    z_codes[:, words].bitcast(FP8X4),
+                    z_scales[:, words],
+                    z_grouped[:, u, W_HALF * half : W_HALF * (half + 1)],
+                )
 
         cv_ps = product("cv_ps", 0, (z_codes, z_scales), (z2_codes, z2_scales))
         cv_win = []
         for u in range(PACK):
             win = keep.tile([P, H], F32, name=f"cv_win{u}")
-            if u == 0:
-                nc.scalar.activation(win[:], cv_ps[u][:], COPY, scale=0.0625)
-            else:
-                nc.vector.tensor_scalar(win[:], cv_ps[u][:], 0.0625, None, ALU.mult)
+            nc.scalar.activation(win[:], cv_ps[u][:], COPY, scale=0.0625)
             cv_win.append(win)
 
         y_codes = keep.tile([P, H], U32, name="y_codes", align_bytes=64)
@@ -202,24 +209,25 @@ def tile_picked_momtmaxbover_none_po_kernel(
             cols = slice(first, first + width)
             entries = slice(first // 16, (first + width) // 16)
             if c == 0:
-                early = keep.tile([P, 2, 2, width], F32, name="early3", tag="held3")
-                rest = keep.tile([P, 2, 2, width], F32, name="rest3")
-                at = [[(early if u < 2 else rest)[:, u % 2, k, :] for k in range(2)] for u in range(PACK)]
+                early = keep.tile([P, PACK, 2, width], F32, name="early3")
+                pairs = [early[:, 0:2], early[:, 2:4]]
             else:
                 if c == 1:
-                    later = keep.tile([P, 2, PACK, 2, width], F32, name="later3", tag="held3")
-                at = [[later[:, c - 1, u, k, :] for k in range(2)] for u in range(PACK)]
+                    later = keep.tile([P, 2, PACK, 2, width], F32, name="later3", tag="z2_codes", align_bytes=64)
+                pairs = [later[:, c - 1, 0:2], later[:, c - 1, 2:4]]
             for u in range(PACK):
                 for k, offsets in enumerate((n3_t, n4_t)):
                     looked_up = cv_win[u][:].indirect(offsets[:, entries])
-                    if (c == 0 and u == 3) or (c == 2 and u == 0 and k == 0):
-                        nc.vector.tensor_copy(at[u][k], looked_up)
+                    if (c == 0 and u < 2) or (c == 1 and u == 0):
+                        nc.vector.tensor_copy(pairs[u // 2][:, u % 2, k, :], looked_up)
                     else:
-                        nc.scalar.activation(at[u][k], looked_up, COPY)
+                        nc.scalar.activation(pairs[u // 2][:, u % 2, k, :], looked_up, COPY)
             larger = keep.tile([P, PACK, width], F32, name=f"larger{c}")
             y = keep.tile([P, PACK, width], F32, name=f"y{c}")
-            for u in range(PACK):
-                nc.vector.tensor_tensor(larger[:, u, :], at[u][0], at[u][1], ALU.max)
+            for h in range(2):
+                nc.vector.tensor_tensor(
+                    larger[:, 2 * h : 2 * h + 2, :], pairs[h][:, :, 0, :], pairs[h][:, :, 1, :], ALU.max
+                )
             for u in range(PACK):
                 nc.vector.scalar_tensor_tensor(
                     y[:, u, :], cv_ps[u][:, cols], -0.75 * 0.0625, larger[:, u, :], ALU.mult, ALU.add

from contextlib import ExitStack

import concourse.mybir as mybir
from concourse.masks import make_identity

K, T, S, H = 512, 2048, 512, 512
FLOPS = 2 * K * S * H * 2 + 2 * S * H * H

F32 = mybir.dt.float32
BF16 = mybir.dt.bfloat16
I32 = mybir.dt.int32
U32 = mybir.dt.uint32
U16 = mybir.dt.uint16
U8 = mybir.dt.uint8
FP8X4 = mybir.dt.float8_e4m3fn_x4
ALU = mybir.AluOpType
COPY = mybir.ActivationFunctionType.Copy

P = 128
PACK = 4
QUARTER = 128
STRIP = 64
CHUNKS = ((0, 256), (256, 128), (384, 128))
W_HALF = H // 2


def tile_picked_momtmaxbover_none_po_kernel(
    tc, x_words, x_scales, wa, wb, gt, gi, offs, two, n1, n2, n3, n4, out_0, out_1, out_2
):
    nc = tc.nc
    with ExitStack() as ctx:
        lists = ctx.enter_context(tc.tile_pool(name="lists", bufs=1))
        keep = ctx.enter_context(tc.tile_pool(name="keep", bufs=1))
        psum = ctx.enter_context(tc.psum_pool(name="psum", bufs=1))

        def load_list(name, src):
            tile = lists.tile([P, S // 16], U16, name=name)
            nc.sync.dma_start(tile[:], src)
            return tile

        def load_weight(name, w, first, width):
            raw = keep.tile([P, PACK, width], F32, name=name)
            nc.sync.dma_start(raw[:], w.rearrange("(p j) c -> p j c", j=PACK)[:, :, first : first + width])
            return raw

        xs = keep.tile([P, T], U8, name="xs", align_bytes=64)
        nc.vector.memset(xs[:].bitcast(I32), 0)
        for q in range(4):
            nc.scalar.dma_start(
                xs[32 * q : 32 * q + 4, :].bitcast(I32), x_scales[0, 4 * q : 4 * q + 4, :].bitcast(I32)
            )
        two_t = load_list("two_t", two)
        xw = keep.tile([P, T], U32, name="xw", align_bytes=64)
        nc.sync.dma_start(xw[:].bitcast(I32), x_words[0].rearrange("p n t -> p (n t)").bitcast(I32))
        wb_raw = [load_weight(f"wb_raw{h}", wb, h * W_HALF, W_HALF) for h in range(2)]
        offs_t = load_list("offs_t", offs)
        wa_raw = [load_weight(f"wa_raw{h}", wa, h * W_HALF, W_HALF) for h in range(2)]
        rows = keep.tile([P, P], F32, name="rows")
        nc.gpsimd.memset(rows[:], 0.0)
        for k, g in enumerate((gt, gi)):
            nc.gpsimd.dma_start(
                rows[PACK * k : PACK * (k + 1), :].rearrange("t (b r) -> t b r", r=8),
                g.rearrange("(b t r) o -> t b (r o)", t=PACK, r=8),
            )
        n2_t = load_list("n2_t", n2)
        n1_t = load_list("n1_t", n1)
        n3_t = load_list("n3_t", n3)
        n4_t = load_list("n4_t", n4)

        ident = keep.tile([P, P], F32, name="ident")
        make_identity(nc, ident[:])
        turned = psum.tile([P, P], F32, name="turned", tag="bank7")
        nc.tensor.transpose(turned[:], rows[:], ident[:])
        gains = keep.tile([P, 2 * PACK], F32, name="gains")
        nc.scalar.copy(gains[:], turned[:, 0 : 2 * PACK])

        def pick(name, table, dtype, offsets, tag):
            picked = keep.tile([P, S], dtype, name=name, tag=tag, align_bytes=64)
            nc.vector.tensor_copy(
                picked[:].rearrange("p (t b r) -> p b t r", t=PACK, r=8), table[:].indirect(offsets[:])
            )
            return picked

        def quantise_weight(name, raws, copies):
            codes = keep.tile([P, H], U32, name=name + "_codes", tag=name + "_codes", align_bytes=64)
            scales = keep.tile([P, H], U8, name=name + "_scales", align_bytes=64)
            width = H // len(raws)
            for piece, raw in enumerate(raws):
                grouped = keep.tile([P, width * PACK], BF16, name=f"{name}_grouped{piece}", tag=f"{name}_grouped{piece}", align_bytes=64)
                copies[piece](
                    grouped[:].rearrange("p (c i j) -> p c j i", i=4, j=PACK),
                    raw[:].rearrange("p j (c i) -> p c j i", i=4),
                )
                cols = slice(piece * width, (piece + 1) * width)
                nc.vector.quantize_mx(codes[:, cols].bitcast(FP8X4), scales[:, cols], grouped[:])
            return codes, scales

        def product(name, first_bank, lhs, rhs):
            banks = []
            for t in range(PACK):
                acc = psum.tile([P, H], F32, name=f"{name}{t}", tag=f"bank{first_bank + t}")
                cols = slice(t * P, (t + 1) * P)
                nc.tensor.matmul_mx(
                    out=acc[:],
                    lhsT=lhs[0][:, cols].bitcast(FP8X4),
                    lhsT_scale=lhs[1][:, cols],
                    rhs=rhs[0][:].bitcast(FP8X4),
                    rhs_scale=rhs[1][:],
                    start=True,
                    stop=True,
                )
                banks.append(acc)
            return banks

        two_scales = pick("two_scales", xs, U8, two_t, "two_scales")
        two_words = pick("two_words", xw, U32, two_t, "two_words")
        idx_scales = pick("idx_scales", xs, U8, offs_t, "idx_scales")
        wb_q = quantise_weight("wb", wb_raw, (nc.scalar.copy, nc.scalar.copy))
        b_ps = product("b_ps", 0, (two_words, two_scales), wb_q)
        idx_words = pick("idx_words", xw, U32, offs_t, "wb_grouped1")
        wa_q = quantise_weight("wa", wa_raw, (nc.scalar.copy, nc.vector.tensor_copy))
        a_ps = product("a_ps", 4, (idx_words, idx_scales), wa_q)

        b_all = keep.tile([P, PACK, H], F32, name="b_all")
        a_all = keep.tile([P, PACK, H], F32, name="a_all")
        for t in range(PACK):
            nc.scalar.copy(b_all[:, t, :], b_ps[t][:])

        z2_grouped = keep.tile([P, H * PACK], BF16, name="z2_grouped", align_bytes=64)
        z2_codes = keep.tile([P, H], U32, name="z2_codes", tag="z2_codes", align_bytes=64)
        z2_scales = keep.tile([P, H], U8, name="z2_scales", align_bytes=64)
        z_grouped = keep.tile([P, PACK, P * PACK], BF16, name="z_grouped", align_bytes=64)
        z_codes = keep.tile([P, H], U32, name="z_codes", align_bytes=64)
        z_scales = keep.tile([P, H], U8, name="z_scales", align_bytes=64)

        def look_up(out, table, offsets, first, width, slots):
            for t in slots:
                entries = offsets[:, first // 16 : (first + width) // 16]
                nc.scalar.activation(out[:, t, :], table[:, t, :].indirect(entries), COPY)

        def weigh_b(first, width):
            nc.gpsimd.tensor_tensor(
                z2_grouped[:, first * PACK : (first + width) * PACK].rearrange("p (c i t) -> p c t i", i=4, t=PACK),
                b_all[:, :, first : first + width].rearrange("p t (c i) -> p c t i", i=4),
                gains[:, PACK : 2 * PACK].unsqueeze(1).unsqueeze(3).to_broadcast([P, width // 4, PACK, 4]),
                ALU.mult,
            )

        b_at0 = keep.tile([P, PACK, W_HALF], F32, name="b_at0")
        look_up(b_at0, b_all, n2_t, 0, W_HALF, range(PACK))
        weigh_b(0, H)
        for t in range(PACK):
            nc.vector.tensor_copy(a_all[:, t, :], a_ps[t][:])
        b_at1 = keep.tile([P, PACK, W_HALF], F32, name="b_at1", tag="wa_codes", align_bytes=64)
        for half, b_at in enumerate((b_at0, b_at1)):
            if half == 1:
                look_up(b_at1, b_all, n2_t, W_HALF, W_HALF, range(PACK))
            upper = keep.tile([P, PACK, W_HALF], F32, name=f"upper{half}")
            cols = slice(half * W_HALF, (half + 1) * W_HALF)
            if half == 0:
                for t in range(PACK):
                    nc.vector.tensor_tensor(upper[:, t, :], a_ps[t][:, cols], b_at[:, t, :], ALU.max)
            else:
                nc.vector.tensor_tensor(upper[:], a_all[:, :, cols], b_at[:], ALU.max)
            if half == 0:
                nc.vector.quantize_mx(z2_codes[:].bitcast(FP8X4), z2_scales[:], z2_grouped[:])
            for quarter in range(2):
                first = half * W_HALF + quarter * QUARTER
                a_at = keep.tile([P, PACK, QUARTER], F32, name=f"a_at{half}{quarter}")
                look_up(a_at, a_all, n1_t, first, QUARTER, range(PACK))
                lower = keep.tile([P, 2, PACK, STRIP], F32, name=f"lower{half}{quarter}")
                spread = keep.tile([P, 2, PACK, STRIP], F32, name=f"spread{half}{quarter}")
                for s in range(2):
                    at = first + s * STRIP
                    nc.vector.tensor_tensor(
                        lower[:, s], b_all[:, :, at : at + STRIP], a_at[:, :, s * STRIP : (s + 1) * STRIP], ALU.min
                    )
                for s in range(2):
                    at = quarter * QUARTER + s * STRIP
                    nc.vector.tensor_tensor(spread[:, s], upper[:, :, at : at + STRIP], lower[:, s], ALU.subtract)
                for s in range(2):
                    at = first + s * STRIP
                    nc.vector.tensor_tensor(
                        z_grouped[:, :, at : at + STRIP].rearrange("p u (m t) -> p m t u", t=PACK),
                        spread[:, s].rearrange("p t (m u) -> p m t u", u=PACK),
                        gains[:, 0:PACK].unsqueeze(1).unsqueeze(3).to_broadcast([P, STRIP // PACK, PACK, PACK]),
                        ALU.mult,
                    )
            for u in range(PACK):
                words = slice(u * P + 64 * half, u * P + 64 * (half + 1))
                nc.vector.quantize_mx(
                    z_codes[:, words].bitcast(FP8X4),
                    z_scales[:, words],
                    z_grouped[:, u, W_HALF * half : W_HALF * (half + 1)],
                )

        cv_ps = product("cv_ps", 0, (z_codes, z_scales), (z2_codes, z2_scales))
        cv_win = []
        for u in range(PACK):
            win = keep.tile([P, H], F32, name=f"cv_win{u}")
            nc.scalar.activation(win[:], cv_ps[u][:], COPY, scale=0.0625)
            cv_win.append(win)

        y_codes = keep.tile([P, H], U32, name="y_codes", align_bytes=64)
        y_scales = keep.tile([P, H], U8, name="y_scales", align_bytes=64)
        y_rows = out_0.rearrange("(p u) c -> p u c", u=PACK)
        y_words = out_1[0].rearrange("p n t -> p (n t)").bitcast(I32)
        for c, (first, width) in enumerate(CHUNKS):
            cols = slice(first, first + width)
            entries = slice(first // 16, (first + width) // 16)
            if c == 0:
                early = keep.tile([P, PACK, 2, width], F32, name="early3")
                pairs = [early[:, 0:2], early[:, 2:4]]
            else:
                if c == 1:
                    later = keep.tile([P, 2, PACK, 2, width], F32, name="later3", tag="z2_codes", align_bytes=64)
                pairs = [later[:, c - 1, 0:2], later[:, c - 1, 2:4]]
            for u in range(PACK):
                for k, offsets in enumerate((n3_t, n4_t)):
                    looked_up = cv_win[u][:].indirect(offsets[:, entries])
                    if (c == 0 and u < 2) or (c == 1 and u == 0):
                        nc.vector.tensor_copy(pairs[u // 2][:, u % 2, k, :], looked_up)
                    else:
                        nc.scalar.activation(pairs[u // 2][:, u % 2, k, :], looked_up, COPY)
            larger = keep.tile([P, PACK, width], F32, name=f"larger{c}")
            y = keep.tile([P, PACK, width], F32, name=f"y{c}")
            for h in range(2):
                nc.vector.tensor_tensor(
                    larger[:, 2 * h : 2 * h + 2, :], pairs[h][:, :, 0, :], pairs[h][:, :, 1, :], ALU.max
                )
            for u in range(PACK):
                nc.vector.scalar_tensor_tensor(
                    y[:, u, :], cv_ps[u][:, cols], -0.75 * 0.0625, larger[:, u, :], ALU.mult, ALU.add
                )
            nc.sync.dma_start(y_rows[:, :, cols], y[:])
            y_grouped = keep.tile([P, width * PACK], BF16, name=f"y_grouped{c}", align_bytes=64)
            nc.vector.tensor_copy(
                y_grouped[:].rearrange("p (c i u) -> p c u i", i=4, u=PACK),
                y[:].rearrange("p u (c i) -> p c u i", i=4),
            )
            nc.vector.quantize_mx(y_codes[:, cols].bitcast(FP8X4), y_scales[:, cols], y_grouped[:])
            engine = nc.scalar if c == len(CHUNKS) - 1 else nc.sync
            engine.dma_start(y_words[:, cols], y_codes[:, cols].bitcast(I32))
        for q in range(4):
            engine = nc.scalar if q % 2 else nc.sync
            engine.dma_start(
                out_2[0, 4 * q : 4 * q + 4, :].bitcast(I32), y_scales[32 * q : 32 * q + 4, :].bitcast(I32)
            )
